import numpy as np
import ml_dtypes


def mxq(x, axis, fmt="e4m3"):
    dtype, down = {"e4m3": (ml_dtypes.float8_e4m3fn, 7), "e5m2": (ml_dtypes.float8_e5m2, 14)}[fmt]
    v = np.moveaxis(np.asarray(x, np.float32).astype(ml_dtypes.bfloat16).astype(np.float64), axis, -1)
    blocks = v.reshape(v.shape[:-1] + (-1, 32))
    amax = np.abs(blocks).max(-1, keepdims=True)
    byte = np.maximum(np.where(amax > 0, np.frexp(amax)[1] - 1 + 127, 0) - down, 1)
    scale = np.exp2(byte - 127.0)
    codes = (blocks / scale).astype(np.float32).astype(dtype).astype(np.float64)
    return np.moveaxis((codes * scale).reshape(v.shape), -1, axis)


WIDE = False


def mx_kscale(k):
    if not WIDE:
        return np.ones(k)
    levels = np.array([24, -24, 12, -12, 0])
    if k % 512:
        return np.exp2(np.random.permutation(np.resize(levels, k // 32))).repeat(32)
    a = np.empty((k // 512, 16))
    for p in range(k // 512):
        a[p, :8] = np.random.permutation(np.resize(levels, 8))
        for g in range(8):
            far = levels[np.abs(levels - a[p, g]) >= 10]
            a[p, g + 8] = far[np.random.randint(len(far))]
    return np.exp2(a.ravel()).repeat(32)


def f64(x):
    return np.asarray(x).astype(np.float64)


def striped(idx):
    return np.tile(idx.reshape(-1, 16).T, (8, 1)).astype(np.uint16)


def unstriped(offs):
    return offs[:16].T.reshape(-1).astype(np.int64)


E2M1 = np.array([0.0, 0.5, 1.0, 1.5, 2.0, 3.0, 4.0, 6.0, -0.0, -0.5, -1.0, -1.5, -2.0, -3.0, -4.0, -6.0])


def pack_weight(w, fmt):
    k, n = w.shape
    w = f64(np.asarray(w, np.float32).astype(ml_dtypes.bfloat16)).reshape(k // 32, 32, n)
    amax = np.abs(w).max(1)
    if fmt == "e4m3":
        byte = np.frexp(amax)[1] - 1 + 127 - 7
    else:
        mant, ex = np.frexp(amax / 6.0)
        byte = np.where(mant > 0.5, ex, ex - 1) + 127
    byte = np.clip(np.where(amax > 0, byte, 1), 1, 254)
    scaled = (w * np.exp2(127.0 - byte)[:, None, :]).reshape(k, n).astype(np.float32)
    by_word = np.ascontiguousarray(scaled.reshape(k // 512, 128, 4, n).transpose(0, 1, 3, 2))
    if fmt == "e4m3":
        words = by_word.astype(ml_dtypes.float8_e4m3fn).view(np.uint8)
    else:
        c = by_word.astype(ml_dtypes.float4_e2m1fn).view(np.uint8) & 0xF
        words = (c[..., 0::2] | (c[..., 1::2] << 4)).reshape(k // 512, 128, 2 * n)
    return np.ascontiguousarray(words), np.ascontiguousarray(byte.astype(np.uint8).reshape(k // 512, 16, n))


def unpack_weight(words, scales, fmt):
    g, _, n = scales.shape
    words = np.ascontiguousarray(words).reshape(g, 128, n, -1)
    if fmt == "e4m3":
        vals = words.view(ml_dtypes.float8_e4m3fn).astype(np.float64)
    else:
        nib = np.empty((g, 128, n, 4), np.uint8)
        nib[..., 0::2] = words & 0xF
        nib[..., 1::2] = words >> 4
        vals = E2M1[nib]
    vals = vals * np.repeat(np.exp2(scales.astype(np.float64) - 127.0), 8, axis=1)[..., None]
    return vals.transpose(0, 1, 3, 2).reshape(g * 512, n)


def gelu(f):
    return 0.5 * f * (1.0 + np.tanh(np.sqrt(2.0 / np.pi) * (f + 0.044715 * f**3)))


K, L, N, T, J = 512, 1024, 512, 4096, 512


def setup_inputs():
    n = np.random.standard_normal
    s = mx_kscale(K)[:, None]
    s2 = mx_kscale(L)[:, None]
    p_tab = pack_weight(n((K, T)) * s, "e4m3")
    return {
        "tab_words": p_tab[0],
        "tab_scales": p_tab[1],
        "w": (n((K, N)) / np.sqrt(K) / s).astype(np.float32),
        "x": (n((L, J)) * s2).astype(np.float32),
        "wx": (n((L, N)) / np.sqrt(L) / s2).astype(np.float32),
        "iw0": (np.random.uniform(0.1, 0.6, J)).astype(np.float32),
        "iw1": (np.random.uniform(0.1, 0.6, J)).astype(np.float32),
        "iw2": (np.random.uniform(0.1, 0.6, J)).astype(np.float32),
        "b": (0.3 * n(N)).astype(np.float32),
        "offs": striped(np.concatenate([np.random.permutation(T)[:J] for _ in range(3)])),
    }


def reference(tab_words, tab_scales, w, x, wx, iw0, iw1, iw2, b, offs):
    idx = unstriped(offs).reshape(3, J)
    tab_ = unpack_weight(tab_words, tab_scales, "e4m3")[:, idx]
    w_ = mxq(f64(w), 0, "e4m3")
    a0 = w_.T @ tab_[:, 0]
    a1 = w_.T @ tab_[:, 1]
    a2 = w_.T @ tab_[:, 2]
    x_ = mxq(f64(x), 0, "e4m3")
    wx_ = mxq(f64(wx), 0, "e4m3")
    ax = wx_.T @ x_
    return gelu(a0 * f64(iw0)[None, :] + a1 * f64(iw1)[None, :] + a2 * f64(iw2)[None, :] + ax + f64(b)[:, None])

@@ -1,0 +1,203 @@
+from contextlib import ExitStack
+
+import concourse.mybir as mybir
+
+K, L, N, T, J = 512, 1024, 512, 4096, 512
+G = 3
+FLOPS = 2 * N * J * (G * K + L)
+
+F32 = mybir.dt.float32
+BF16 = mybir.dt.bfloat16
+I32 = mybir.dt.int32
+U32 = mybir.dt.uint32
+U16 = mybir.dt.uint16
+U8 = mybir.dt.uint8
+FP8X4 = mybir.dt.float8_e4m3fn_x4
+ACT = mybir.ActivationFunctionType
+ADD = mybir.AluOpType.add
+
+P = 128
+PACK = 4
+K_PASS = P * PACK
+BLOCKS = 4
+HALF = N // 2
+
+
+def tile_list_interp_gelu_kernel(
+    tc, tab_words, tab_scales, w, x, wx, iw0, iw1, iw2, b, offs, out
+):
+    nc = tc.nc
+    with ExitStack() as ctx:
+        keep = ctx.enter_context(tc.tile_pool(name="keep", bufs=1))
+        ring = ctx.enter_context(tc.tile_pool(name="ring", bufs=4))
+        sums = ctx.enter_context(tc.psum_pool(name="sums", bufs=1))
+        prods = ctx.enter_context(tc.psum_pool(name="prods", bufs=4))
+
+        def load_rows(name, rows, tag):
+            raw = keep.tile([P, PACK, rows.shape[1]], F32, name=name + "_raw", tag=tag, align_bytes=64)
+            nc.sync.dma_start(out=raw[:], in_=rows.rearrange("(p t) c -> p t c", t=PACK))
+            return raw
+
+        def interleave(name, raw, copy):
+            width = raw.shape[2]
+            grouped = keep.tile([P, width, PACK], BF16, name=name + "_bf16", tag=name + "_bf16", align_bytes=64)
+            copy(
+                out=grouped[:].rearrange("p (c i) t -> p c t i", i=4),
+                in_=raw[:].rearrange("p t (c i) -> p c t i", i=4),
+            )
+            return grouped
+
+        def quantize(name, grouped):
+            width = grouped.shape[1]
+            codes = keep.tile([P, width], U32, name=name + "_codes", align_bytes=64)
+            scales = keep.tile([P, width], U8, name=name + "_scales", align_bytes=64)
+            nc.vector.quantize_mx(
+                out=codes[:].bitcast(FP8X4),
+                scales=scales[:],
+                in_=grouped[:].rearrange("p c t -> p (c t)"),
+            )
+            return codes, scales
+
+        def product(acc, lhs, lhs_cols, rhs, rhs_cols, start, stop):
+            nc.tensor.matmul_mx(
+                out=acc,
+                lhsT=lhs[0][:, lhs_cols].bitcast(FP8X4),
+                lhsT_scale=lhs[1][:, lhs_cols],
+                rhs=rhs[0][:, rhs_cols].bitcast(FP8X4),
+                rhs_scale=rhs[1][:, rhs_cols],
+                start=start,
+                stop=stop,
+            )
+
+        def block(i):
+            return slice(i * P, (i + 1) * P)
+
+        offsets = keep.tile([P, G * J // 16], U16, name="offsets")
+        nc.sync.dma_start(offsets[:], offs)
+        w_raw = load_rows("w", w, "w_raw")
+
+        zero_in = keep.tile([P, 1], F32, name="zero_in", tag="x0_raw", align_bytes=64)
+        nc.vector.memset(zero_in[:], 0.0)
+        zero = keep.tile([P, 1], F32, name="zero")
+        nc.scalar.activation(zero[:], zero_in[:], ACT.Gelu_apprx_tanh)
+
+        table_scales = keep.tile([P, T], U8, name="table_scales", tag="table_scales", align_bytes=64)
+        nc.vector.memset(table_scales[:].bitcast(I32), 0)
+        for q in range(4):
+            nc.sync.dma_start(
+                out=table_scales[32 * q : 32 * q + 4, :].bitcast(I32),
+                in_=tab_scales[0, 4 * q : 4 * q + 4, :].bitcast(I32),
+            )
+
+        zeros = keep.tile([P, P], F32, name="zeros", tag="table_words", align_bytes=64)
+        nc.vector.memset(zeros[:], 0.0)
+        ident = keep.tile([P, P], F32, name="ident")
+        nc.gpsimd.affine_select(
+            out=ident[:],
+            in_=zeros[:],
+            compare_op=mybir.AluOpType.not_equal,
+            fill=1.0,
+            base=0,
+            pattern=[[-1, P]],
+            channel_multiplier=1,
+        )
+        rows = keep.tile([P, P], F32, name="rows")
+        nc.gpsimd.tensor_scalar(rows[:], zeros[:], 1.0, 0.0, mybir.AluOpType.mult, ADD)
+
+        table_words = keep.tile([P, T], I32, name="table_words", tag="table_words", align_bytes=64)
+        nc.sync.dma_start(out=table_words[:], in_=tab_words[0].rearrange("p t i -> p (t i)").bitcast(I32))
+        for r, vec in enumerate((iw0, iw1, iw2, b)):
+            nc.sync.dma_start(out=rows[BLOCKS * r : BLOCKS * (r + 1), :], in_=vec.rearrange("(c p) -> c p", p=P))
+        x_raw = [load_rows("x0", x[0:K_PASS, :], "x0_raw")]
+
+        picked_scales = keep.tile([P, G * J], U8, name="picked_scales", align_bytes=64)
+        nc.vector.tensor_copy(picked_scales[:], table_scales[:].indirect(offsets[:]))
+        w_mx = quantize("w", interleave("w", w_raw, nc.scalar.copy))
+
+        turned = prods.tile([P, N], F32, name="prod")
+        nc.tensor.transpose(turned[:, 0:P], rows[:], ident[:])
+        cols = keep.tile([P, 4 * BLOCKS], F32, name="cols")
+        nc.scalar.copy(cols[:], turned[:, 0 : 4 * BLOCKS])
+
+        total = [sums.tile([P, J], F32, name="total%d" % nb) for nb in range(BLOCKS)]
+
+        for g in range(G):
+            words = keep.tile([P, J], U32, name="picked_words%d" % g, align_bytes=64)
+            nc.vector.tensor_copy(
+                words[:], table_words[:].bitcast(U32).indirect(offsets[:, g * J // 16 : (g + 1) * J // 16])
+            )
+            picked = (words, picked_scales[:, g * J : (g + 1) * J])
+            scaled = []
+            for jb in range(BLOCKS):
+                acc = prods.tile([P, N], F32, name="prod")
+                product(acc[:], picked, block(jb), w_mx, slice(0, N), True, True)
+                term = ring.tile([P, N], F32, name="term", bufs=8)
+                nc.scalar.activation(
+                    term[:], acc[:], ACT.Identity, bias=zero[:], scale=cols[:, BLOCKS * g + jb : BLOCKS * g + jb + 1]
+                )
+                scaled.append(term)
+            for jb in range(BLOCKS):
+                for nb in range(BLOCKS):
+                    nc.tensor.matmul(
+                        total[nb][:, block(jb)],
+                        scaled[jb][:, block(nb)],
+                        ident[:],
+                        is_transpose=True,
+                        start=(g == 0 and jb == 0),
+                        stop=(nb >= 2 and g == G - 1 and jb == BLOCKS - 1),
+                    )
+
+        def load_wx(h, a, tag):
+            return load_rows("wx%d%d" % (h, a), wx[a * K_PASS : (a + 1) * K_PASS, h * HALF : (h + 1) * HALF], tag)
+
+        x_raw.append(load_rows("x1", x[K_PASS:L, :], "w_raw"))
+        wx_raw = [[load_wx(0, 0, "table_scales"), load_wx(0, 1, "w_bf16"), ], [load_wx(1, 0, "table_words")]]
+        x_bf = [interleave("x%d" % a, x_raw[a], nc.vector.tensor_copy) for a in range(2)]
+        wx_raw[1].append(load_wx(1, 1, "x0_raw"))
+        x_mx = [quantize("x%d" % a, x_bf[a]) for a in range(2)]
+        wx_mx = []
+        for h in range(2):
+            bf = [interleave("wx%d%d" % (h, a), wx_raw[h][a], nc.vector.tensor_copy) for a in range(2)]
+            wx_mx.append([quantize("wx%d%d" % (h, a), bf[a]) for a in range(2)])
+
+        def finish(nb, source):
+            result = ring.tile([P, J], F32, name="result")
+            nc.scalar.activation(
+                result[:], source, ACT.Gelu_apprx_tanh, bias=cols[:, BLOCKS * G + nb : BLOCKS * G + nb + 1]
+            )
+            nc.sync.dma_start(out=out[block(nb), :], in_=result[:])
+
+        interp = []
+        for nb in (2, 3):
+            held = keep.tile([P, J], F32, name="interp%d" % nb)
+            nc.scalar.copy(held[:], total[nb][:])
+            interp.append(held)
+
+        for pair in range(2):
+            acc = prods.tile([P, N], F32, name="prod")
+            for u in range(2):
+                for a in range(2):
+                    product(acc[:, u * HALF : (u + 1) * HALF], x_mx[a], block(2 * pair + u), wx_mx[0][a], slice(0, HALF), a == 0, a == 1)
+            term = ring.tile([P, N], F32, name="term", bufs=8)
+            nc.scalar.copy(term[:], acc[:])
+            for u in range(2):
+                for nb in range(2):
+                    nc.tensor.matmul(
+                        total[nb][:, block(2 * pair + u)],
+                        term[:, u * HALF + nb * P : u * HALF + (nb + 1) * P],
+                        ident[:],
+                        is_transpose=True,
+                        start=False,
+                        stop=(pair == 1 and u == 1),
+                    )
+        for nb in range(2):
+            finish(nb, total[nb][:])
+
+        accs = [prods.tile([P, J], F32, name="prod") for nb in (2, 3)]
+        for a in range(2):
+            for i in range(2):
+                product(accs[i][:], wx_mx[1][a], block(i), x_mx[a], slice(0, J), a == 0, a == 1)
+        for i in range(2):
+            both = ring.tile([P, J], F32, name="both")
+            nc.vector.tensor_tensor(both[:], accs[i][:], interp[i][:], ADD)
+            finish(2 + i, both[:])

@@ -1,6 +1,7 @@
 from contextlib import ExitStack
 
 import concourse.mybir as mybir
+from concourse.masks import make_identity
 
 K, L, N, T, J = 512, 1024, 512, 4096, 512
 G = 3
@@ -15,12 +16,14 @@ U8 = mybir.dt.uint8
 FP8X4 = mybir.dt.float8_e4m3fn_x4
 ACT = mybir.ActivationFunctionType
 ADD = mybir.AluOpType.add
+MULT = mybir.AluOpType.mult
 
 P = 128
 PACK = 4
 K_PASS = P * PACK
 BLOCKS = 4
 HALF = N // 2
+MERGED = ((1, 0), (1, 1), (1, 2), (1, 3))
 
 
 def tile_list_interp_gelu_kernel(
@@ -32,6 +35,8 @@ def tile_list_interp_gelu_kernel(
         ring = ctx.enter_context(tc.tile_pool(name="ring", bufs=4))
         sums = ctx.enter_context(tc.psum_pool(name="sums", bufs=1))
         prods = ctx.enter_context(tc.psum_pool(name="prods", bufs=4))
+        on_vector = nc.vector.tensor_copy
+        on_scalar = nc.scalar.copy
 
         def load_rows(name, rows, tag):
             raw = keep.tile([P, PACK, rows.shape[1]], F32, name=name + "_raw", tag=tag, align_bytes=64)
@@ -47,16 +52,17 @@ def tile_list_interp_gelu_kernel(
             )
             return grouped
 
-        def quantize(name, grouped):
-            width = grouped.shape[1]
+        def operand(name, width):
             codes = keep.tile([P, width], U32, name=name + "_codes", align_bytes=64)
             scales = keep.tile([P, width], U8, name=name + "_scales", align_bytes=64)
+            return codes, scales
+
+        def quantize(mx, cols, grouped):
             nc.vector.quantize_mx(
-                out=codes[:].bitcast(FP8X4),
-                scales=scales[:],
+                out=mx[0][:, cols].bitcast(FP8X4),
+                scales=mx[1][:, cols],
                 in_=grouped[:].rearrange("p c t -> p (c t)"),
             )
-            return codes, scales
 
         def product(acc, lhs, lhs_cols, rhs, rhs_cols, start, stop):
             nc.tensor.matmul_mx(
@@ -72,132 +78,134 @@ def tile_list_interp_gelu_kernel(
         def block(i):
             return slice(i * P, (i + 1) * P)
 
+        def half(h):
+            return slice(h * HALF, (h + 1) * HALF)
+
+        def probe(name, ap):
+            clock = keep.tile([P, 1], ap.dtype, name=name)
+            nc.gpsimd.tensor_copy(clock[:], ap)
+
         offsets = keep.tile([P, G * J // 16], U16, name="offsets")
         nc.sync.dma_start(offsets[:], offs)
-        w_raw = load_rows("w", w, "w_raw")
+        w_raw = [load_rows("w0", w[:, half(0)], "w0_raw")]
 
-        zero_in = keep.tile([P, 1], F32, name="zero_in", tag="x0_raw", align_bytes=64)
-        nc.vector.memset(zero_in[:], 0.0)
-        zero = keep.tile([P, 1], F32, name="zero")
-        nc.scalar.activation(zero[:], zero_in[:], ACT.Gelu_apprx_tanh)
+        rows = keep.tile([P, P], F32, name="rows")
+        nc.gpsimd.memset(rows[:], 0.0)
+        for r, vec in enumerate((iw0, iw1, iw2, b)):
+            nc.sync.dma_start(out=rows[BLOCKS * r : BLOCKS * (r + 1), :], in_=vec.rearrange("(c p) -> c p", p=P))
+        ident = keep.tile([P, P], F32, name="ident")
+        make_identity(nc, ident[:])
 
         table_scales = keep.tile([P, T], U8, name="table_scales", tag="table_scales", align_bytes=64)
         nc.vector.memset(table_scales[:].bitcast(I32), 0)
-        for q in range(4):
-            nc.sync.dma_start(
-                out=table_scales[32 * q : 32 * q + 4, :].bitcast(I32),
-                in_=tab_scales[0, 4 * q : 4 * q + 4, :].bitcast(I32),
-            )
+        nc.sync.dma_start(out=table_scales[0:P:8, :].bitcast(I32), in_=tab_scales[0].bitcast(I32))
 
-        zeros = keep.tile([P, P], F32, name="zeros", tag="table_words", align_bytes=64)
-        nc.vector.memset(zeros[:], 0.0)
-        ident = keep.tile([P, P], F32, name="ident")
-        nc.gpsimd.affine_select(
-            out=ident[:],
-            in_=zeros[:],
-            compare_op=mybir.AluOpType.not_equal,
-            fill=1.0,
-            base=0,
-            pattern=[[-1, P]],
-            channel_multiplier=1,
-        )
-        rows = keep.tile([P, P], F32, name="rows")
-        nc.gpsimd.tensor_scalar(rows[:], zeros[:], 1.0, 0.0, mybir.AluOpType.mult, ADD)
+        blank = keep.tile([P, 1], F32, name="blank", tag="table_words", align_bytes=64)
+        nc.vector.memset(blank[:], 0.0)
+        zero_in = keep.tile([P, 1], F32, name="zero_in", tag="w1_raw", align_bytes=64)
+        nc.vector.tensor_copy(zero_in[:], blank[:])
+        zero = keep.tile([P, 1], F32, name="zero")
+        nc.scalar.activation(zero[:], zero_in[:], ACT.Gelu_apprx_tanh)
 
         table_words = keep.tile([P, T], I32, name="table_words", tag="table_words", align_bytes=64)
         nc.sync.dma_start(out=table_words[:], in_=tab_words[0].rearrange("p t i -> p (t i)").bitcast(I32))
-        for r, vec in enumerate((iw0, iw1, iw2, b)):
-            nc.sync.dma_start(out=rows[BLOCKS * r : BLOCKS * (r + 1), :], in_=vec.rearrange("(c p) -> c p", p=P))
-        x_raw = [load_rows("x0", x[0:K_PASS, :], "x0_raw")]
+        w_raw.append(load_rows("w1", w[:, half(1)], "w1_raw"))
 
         picked_scales = keep.tile([P, G * J], U8, name="picked_scales", align_bytes=64)
-        nc.vector.tensor_copy(picked_scales[:], table_scales[:].indirect(offsets[:]))
-        w_mx = quantize("w", interleave("w", w_raw, nc.scalar.copy))
+        nc.vector.memset(picked_scales[:].bitcast(I32), 0)
+        picked_rows = keep.tile([P, G * J], U8, name="picked_rows", tag="picked_rows", align_bytes=64)
+        nc.vector.tensor_copy(picked_rows[:], table_scales[:].indirect(offsets[:]))
+        for r in range(4):
+            nc.scalar.dma_start(out=picked_scales[r:P:32, :].bitcast(I32), in_=picked_rows[8 * r : P : 32, :].bitcast(I32))
+
+        w_mx = (
+            keep.tile([P, N], U32, name="w_codes", tag="table_scales", align_bytes=64),
+            keep.tile([P, N], U8, name="w_scales", align_bytes=64),
+        )
+        quantize(w_mx, half(0), interleave("w0", w_raw[0], on_scalar))
+        x_raw = [load_rows("x0", x[0:K_PASS, :], "w0_bf16")]
 
         turned = prods.tile([P, N], F32, name="prod")
         nc.tensor.transpose(turned[:, 0:P], rows[:], ident[:])
         cols = keep.tile([P, 4 * BLOCKS], F32, name="cols")
         nc.scalar.copy(cols[:], turned[:, 0 : 4 * BLOCKS])
 
-        total = [sums.tile([P, J], F32, name="total%d" % nb) for nb in range(BLOCKS)]
-
-        for g in range(G):
-            words = keep.tile([P, J], U32, name="picked_words%d" % g, align_bytes=64)
+        def gather(g, tag):
+            words = keep.tile([P, J], U32, name="picked_words%d" % g, tag=tag, align_bytes=64)
             nc.vector.tensor_copy(
                 words[:], table_words[:].bitcast(U32).indirect(offsets[:, g * J // 16 : (g + 1) * J // 16])
             )
-            picked = (words, picked_scales[:, g * J : (g + 1) * J])
-            scaled = []
-            for jb in range(BLOCKS):
-                acc = prods.tile([P, N], F32, name="prod")
-                product(acc[:], picked, block(jb), w_mx, slice(0, N), True, True)
-                term = ring.tile([P, N], F32, name="term", bufs=8)
-                nc.scalar.activation(
-                    term[:], acc[:], ACT.Identity, bias=zero[:], scale=cols[:, BLOCKS * g + jb : BLOCKS * g + jb + 1]
+            return words, picked_scales[:, g * J : (g + 1) * J]
+
+        picked = [gather(0, "picked0"), gather(1, "picked1")]
+        quantize(w_mx, half(1), interleave("w1", w_raw[1], on_scalar))
+        picked.append(gather(2, "w1_bf16"))
+
+        wx_raw = [load_rows("wx0", wx[0:K_PASS, :], "picked_rows")]
+        x_raw.append(load_rows("x1", x[K_PASS:L, :], "w1_raw"))
+        wx_raw.append(load_rows("wx10", wx[K_PASS:L, half(0)], "table_words"))
+
+        total = [sums.tile([P, J], F32, name="total%d" % nb) for nb in range(BLOCKS)]
+
+        def weight(g, jb):
+            return cols[:, BLOCKS * g + jb : BLOCKS * g + jb + 1]
+
+        def add_turned(term, jb, first, last):
+            for nb in range(BLOCKS):
+                nc.tensor.matmul(
+                    total[nb][:, block(jb)],
+                    term[:, block(nb)],
+                    ident[:],
+                    is_transpose=True,
+                    start=first,
+                    stop=last,
                 )
-                scaled.append(term)
+
+        def project(g, jb):
+            acc = prods.tile([P, N], F32, name="prod")
+            product(acc[:], picked[g], block(jb), w_mx, slice(0, N), True, True)
+            return acc
+
+        x_mx = [operand("x%d" % a, J) for a in range(2)]
+        wx_mx = [operand("wx%d" % a, N) for a in range(2)]
+
+        terms = {}
+        waiting = []
+        for g in range(G):
             for jb in range(BLOCKS):
-                for nb in range(BLOCKS):
-                    nc.tensor.matmul(
-                        total[nb][:, block(jb)],
-                        scaled[jb][:, block(nb)],
-                        ident[:],
-                        is_transpose=True,
-                        start=(g == 0 and jb == 0),
-                        stop=(nb >= 2 and g == G - 1 and jb == BLOCKS - 1),
-                    )
+                acc = project(g, jb)
+                term = ring.tile([P, N], F32, name="term", bufs=12)
+                if (g, jb) in MERGED:
+                    nc.vector.scalar_tensor_tensor(term[:], acc[:], weight(g, jb), terms[g - 1, jb][:], MULT, ADD)
+                else:
+                    nc.scalar.activation(term[:], acc[:], ACT.Identity, bias=zero[:], scale=weight(g, jb))
+                terms[g, jb] = term
+                if (g + 1, jb) not in MERGED:
+                    waiting.append((term, jb))
+        for i, (term, jb) in enumerate(waiting):
+            add_turned(term, jb, i == 0, i == len(waiting) - 1)
 
-        def load_wx(h, a, tag):
-            return load_rows("wx%d%d" % (h, a), wx[a * K_PASS : (a + 1) * K_PASS, h * HALF : (h + 1) * HALF], tag)
-
-        x_raw.append(load_rows("x1", x[K_PASS:L, :], "w_raw"))
-        wx_raw = [[load_wx(0, 0, "table_scales"), load_wx(0, 1, "w_bf16"), ], [load_wx(1, 0, "table_words")]]
-        x_bf = [interleave("x%d" % a, x_raw[a], nc.vector.tensor_copy) for a in range(2)]
-        wx_raw[1].append(load_wx(1, 1, "x0_raw"))
-        x_mx = [quantize("x%d" % a, x_bf[a]) for a in range(2)]
-        wx_mx = []
-        for h in range(2):
-            bf = [interleave("wx%d%d" % (h, a), wx_raw[h][a], nc.vector.tensor_copy) for a in range(2)]
-            wx_mx.append([quantize("wx%d%d" % (h, a), bf[a]) for a in range(2)])
-
-        def finish(nb, source):
-            result = ring.tile([P, J], F32, name="result")
-            nc.scalar.activation(
-                result[:], source, ACT.Gelu_apprx_tanh, bias=cols[:, BLOCKS * G + nb : BLOCKS * G + nb + 1]
-            )
-            nc.sync.dma_start(out=out[block(nb), :], in_=result[:])
+        quantize(x_mx[0], slice(0, J), interleave("x0", x_raw[0], on_vector))
+        wx_raw.append(load_rows("wx11", wx[K_PASS:L, half(1)], "w0_bf16"))
+        quantize(wx_mx[0], slice(0, N), interleave("wx0", wx_raw[0], on_vector))
+        x1_bf = interleave("x1", x_raw[1], on_scalar)
+        quantize(wx_mx[1], half(0), interleave("wx10", wx_raw[1], on_vector))
+        quantize(x_mx[1], slice(0, J), x1_bf)
+        quantize(wx_mx[1], half(1), interleave("wx11", wx_raw[2], on_vector))
 
         interp = []
-        for nb in (2, 3):
+        for nb in range(BLOCKS):
             held = keep.tile([P, J], F32, name="interp%d" % nb)
             nc.scalar.copy(held[:], total[nb][:])
             interp.append(held)
 
-        for pair in range(2):
-            acc = prods.tile([P, N], F32, name="prod")
-            for u in range(2):
-                for a in range(2):
-                    product(acc[:, u * HALF : (u + 1) * HALF], x_mx[a], block(2 * pair + u), wx_mx[0][a], slice(0, HALF), a == 0, a == 1)
-            term = ring.tile([P, N], F32, name="term", bufs=8)
-            nc.scalar.copy(term[:], acc[:])
-            for u in range(2):
-                for nb in range(2):
-                    nc.tensor.matmul(
-                        total[nb][:, block(2 * pair + u)],
-                        term[:, u * HALF + nb * P : u * HALF + (nb + 1) * P],
-                        ident[:],
-                        is_transpose=True,
-                        start=False,
-                        stop=(pair == 1 and u == 1),
-                    )
-        for nb in range(2):
-            finish(nb, total[nb][:])
-
-        accs = [prods.tile([P, J], F32, name="prod") for nb in (2, 3)]
+        accs = [prods.tile([P, J], F32, name="prod") for nb in range(BLOCKS)]
         for a in range(2):
-            for i in range(2):
-                product(accs[i][:], wx_mx[1][a], block(i), x_mx[a], slice(0, J), a == 0, a == 1)
-        for i in range(2):
-            both = ring.tile([P, J], F32, name="both")
-            nc.vector.tensor_tensor(both[:], accs[i][:], interp[i][:], ADD)
-            finish(2 + i, both[:])
+            for nb in range(BLOCKS):
+                product(accs[nb][:], wx_mx[a], block(nb), x_mx[a], slice(0, J), a == 0, a == 1)
+        for nb, js in ((0, slice(0, J)), (1, slice(0, J)), (2, slice(0, J)), (3, half(0)), (3, half(1))):
+            both = ring.tile([P, js.stop - js.start], F32, name="both")
+            nc.vector.tensor_tensor(both[:], accs[nb][:, js], interp[nb][:, js], ADD)
+            result = ring.tile([P, js.stop - js.start], F32, name="result", bufs=6)
+            nc.scalar.activation(result[:], both[:], ACT.Gelu_apprx_tanh, bias=weight(G, nb))
+            nc.sync.dma_start(out=out[block(nb), js], in_=result[:])

@@ -185,12 +185,16 @@ def tile_list_interp_gelu_kernel(
         for i, (term, jb) in enumerate(waiting):
             add_turned(term, jb, i == 0, i == len(waiting) - 1)
 
-        quantize(x_mx[0], slice(0, J), interleave("x0", x_raw[0], on_vector))
+        x0_bf = keep.tile([P, J, PACK], BF16, name="x0_bf16", align_bytes=64)
+        nc.gpsimd.tensor_scalar(x0_bf[:], x_raw[0][:].rearrange("p t c -> p c t"), 1.0, 0.0, MULT, ADD)
+        quantize(x_mx[0], slice(0, J), x0_bf)
         wx_raw.append(load_rows("wx11", wx[K_PASS:L, half(1)], "w0_bf16"))
         quantize(wx_mx[0], slice(0, N), interleave("wx0", wx_raw[0], on_vector))
-        x1_bf = interleave("x1", x_raw[1], on_scalar)
-        quantize(wx_mx[1], half(0), interleave("wx10", wx_raw[1], on_vector))
-        quantize(x_mx[1], slice(0, J), x1_bf)
+        x1_bf = [interleave("x1%d" % h, x_raw[1][:, :, half(h)], (on_vector, on_scalar)[h]) for h in range(2)]
+        quantize(x_mx[1], half(0), x1_bf[0])
+        wx10_bf = interleave("wx10", wx_raw[1], on_vector)
+        quantize(x_mx[1], half(1), x1_bf[1])
+        quantize(wx_mx[1], half(0), wx10_bf)
         quantize(wx_mx[1], half(1), interleave("wx11", wx_raw[2], on_vector))
 
         interp = []

from contextlib import ExitStack

import concourse.mybir as mybir
from concourse.masks import make_identity

K, L, N, T, J = 512, 1024, 512, 4096, 512
G = 3
FLOPS = 2 * N * J * (G * K + L)

F32 = mybir.dt.float32
BF16 = mybir.dt.bfloat16
I32 = mybir.dt.int32
U32 = mybir.dt.uint32
U16 = mybir.dt.uint16
U8 = mybir.dt.uint8
FP8X4 = mybir.dt.float8_e4m3fn_x4
ACT = mybir.ActivationFunctionType
ADD = mybir.AluOpType.add
MULT = mybir.AluOpType.mult

P = 128
PACK = 4
K_PASS = P * PACK
BLOCKS = 4
HALF = N // 2
MERGED = ((1, 0), (1, 1), (1, 2), (1, 3))


def tile_list_interp_gelu_kernel(
    tc, tab_words, tab_scales, w, x, wx, iw0, iw1, iw2, b, offs, out
):
    nc = tc.nc
    with ExitStack() as ctx:
        keep = ctx.enter_context(tc.tile_pool(name="keep", bufs=1))
        ring = ctx.enter_context(tc.tile_pool(name="ring", bufs=4))
        sums = ctx.enter_context(tc.psum_pool(name="sums", bufs=1))
        prods = ctx.enter_context(tc.psum_pool(name="prods", bufs=4))
        on_vector = nc.vector.tensor_copy
        on_scalar = nc.scalar.copy

        def load_rows(name, rows, tag):
            raw = keep.tile([P, PACK, rows.shape[1]], F32, name=name + "_raw", tag=tag, align_bytes=64)
            nc.sync.dma_start(out=raw[:], in_=rows.rearrange("(p t) c -> p t c", t=PACK))
            return raw

        def interleave(name, raw, copy):
            width = raw.shape[2]
            grouped = keep.tile([P, width, PACK], BF16, name=name + "_bf16", tag=name + "_bf16", align_bytes=64)
            copy(
                out=grouped[:].rearrange("p (c i) t -> p c t i", i=4),
                in_=raw[:].rearrange("p t (c i) -> p c t i", i=4),
            )
            return grouped

        def operand(name, width):
            codes = keep.tile([P, width], U32, name=name + "_codes", align_bytes=64)
            scales = keep.tile([P, width], U8, name=name + "_scales", align_bytes=64)
            return codes, scales

        def quantize(mx, cols, grouped):
            nc.vector.quantize_mx(
                out=mx[0][:, cols].bitcast(FP8X4),
                scales=mx[1][:, cols],
                in_=grouped[:].rearrange("p c t -> p (c t)"),
            )

        def product(acc, lhs, lhs_cols, rhs, rhs_cols, start, stop):
            nc.tensor.matmul_mx(
                out=acc,
                lhsT=lhs[0][:, lhs_cols].bitcast(FP8X4),
                lhsT_scale=lhs[1][:, lhs_cols],
                rhs=rhs[0][:, rhs_cols].bitcast(FP8X4),
                rhs_scale=rhs[1][:, rhs_cols],
                start=start,
                stop=stop,
            )

        def block(i):
            return slice(i * P, (i + 1) * P)

        def half(h):
            return slice(h * HALF, (h + 1) * HALF)

        def probe(name, ap):
            clock = keep.tile([P, 1], ap.dtype, name=name)
            nc.gpsimd.tensor_copy(clock[:], ap)

        offsets = keep.tile([P, G * J // 16], U16, name="offsets")
        nc.sync.dma_start(offsets[:], offs)
        w_raw = [load_rows("w0", w[:, half(0)], "w0_raw")]

        rows = keep.tile([P, P], F32, name="rows")
        nc.gpsimd.memset(rows[:], 0.0)
        for r, vec in enumerate((iw0, iw1, iw2, b)):
            nc.sync.dma_start(out=rows[BLOCKS * r : BLOCKS * (r + 1), :], in_=vec.rearrange("(c p) -> c p", p=P))
        ident = keep.tile([P, P], F32, name="ident")
        make_identity(nc, ident[:])

        table_scales = keep.tile([P, T], U8, name="table_scales", tag="table_scales", align_bytes=64)
        nc.vector.memset(table_scales[:].bitcast(I32), 0)
        nc.sync.dma_start(out=table_scales[0:P:8, :].bitcast(I32), in_=tab_scales[0].bitcast(I32))

        blank = keep.tile([P, 1], F32, name="blank", tag="table_words", align_bytes=64)
        nc.vector.memset(blank[:], 0.0)
        zero_in = keep.tile([P, 1], F32, name="zero_in", tag="w1_raw", align_bytes=64)
        nc.vector.tensor_copy(zero_in[:], blank[:])
        zero = keep.tile([P, 1], F32, name="zero")
        nc.scalar.activation(zero[:], zero_in[:], ACT.Gelu_apprx_tanh)

        table_words = keep.tile([P, T], I32, name="table_words", tag="table_words", align_bytes=64)
        nc.sync.dma_start(out=table_words[:], in_=tab_words[0].rearrange("p t i -> p (t i)").bitcast(I32))
        w_raw.append(load_rows("w1", w[:, half(1)], "w1_raw"))

        picked_scales = keep.tile([P, G * J], U8, name="picked_scales", align_bytes=64)
        nc.vector.memset(picked_scales[:].bitcast(I32), 0)
        picked_rows = keep.tile([P, G * J], U8, name="picked_rows", tag="picked_rows", align_bytes=64)
        nc.vector.tensor_copy(picked_rows[:], table_scales[:].indirect(offsets[:]))
        for r in range(4):
            nc.scalar.dma_start(out=picked_scales[r:P:32, :].bitcast(I32), in_=picked_rows[8 * r : P : 32, :].bitcast(I32))

        w_mx = (
            keep.tile([P, N], U32, name="w_codes", tag="table_scales", align_bytes=64),
            keep.tile([P, N], U8, name="w_scales", align_bytes=64),
        )
        quantize(w_mx, half(0), interleave("w0", w_raw[0], on_scalar))
        x_raw = [load_rows("x0", x[0:K_PASS, :], "w0_bf16")]

        turned = prods.tile([P, N], F32, name="prod")
        nc.tensor.transpose(turned[:, 0:P], rows[:], ident[:])
        cols = keep.tile([P, 4 * BLOCKS], F32, name="cols")
        nc.scalar.copy(cols[:], turned[:, 0 : 4 * BLOCKS])

        def gather(g, tag):
            words = keep.tile([P, J], U32, name="picked_words%d" % g, tag=tag, align_bytes=64)
            nc.vector.tensor_copy(
                words[:], table_words[:].bitcast(U32).indirect(offsets[:, g * J // 16 : (g + 1) * J // 16])
            )
            return words, picked_scales[:, g * J : (g + 1) * J]

        picked = [gather(0, "picked0"), gather(1, "picked1")]
        quantize(w_mx, half(1), interleave("w1", w_raw[1], on_scalar))
        picked.append(gather(2, "w1_bf16"))

        wx_raw = [load_rows("wx0", wx[0:K_PASS, :], "picked_rows")]
        x_raw.append(load_rows("x1", x[K_PASS:L, :], "w1_raw"))
        wx_raw.append(load_rows("wx10", wx[K_PASS:L, half(0)], "table_words"))

        total = [sums.tile([P, J], F32, name="total%d" % nb) for nb in range(BLOCKS)]

        def weight(g, jb):
            return cols[:, BLOCKS * g + jb : BLOCKS * g + jb + 1]

        def add_turned(term, jb, first, last):
            for nb in range(BLOCKS):
                nc.tensor.matmul(
                    total[nb][:, block(jb)],
                    term[:, block(nb)],
                    ident[:],
                    is_transpose=True,
                    start=first,
                    stop=last,
                )

        def project(g, jb):
            acc = prods.tile([P, N], F32, name="prod")
            product(acc[:], picked[g], block(jb), w_mx, slice(0, N), True, True)
            return acc

        x_mx = [operand("x%d" % a, J) for a in range(2)]
        wx_mx = [operand("wx%d" % a, N) for a in range(2)]

        terms = {}
        waiting = []
        for g in range(G):
            for jb in range(BLOCKS):
                acc = project(g, jb)
                term = ring.tile([P, N], F32, name="term", bufs=12)
                if (g, jb) in MERGED:
                    nc.vector.scalar_tensor_tensor(term[:], acc[:], weight(g, jb), terms[g - 1, jb][:], MULT, ADD)
                else:
                    nc.scalar.activation(term[:], acc[:], ACT.Identity, bias=zero[:], scale=weight(g, jb))
                terms[g, jb] = term
                if (g + 1, jb) not in MERGED:
                    waiting.append((term, jb))
        for i, (term, jb) in enumerate(waiting):
            add_turned(term, jb, i == 0, i == len(waiting) - 1)

        x0_bf = keep.tile([P, J, PACK], BF16, name="x0_bf16", align_bytes=64)
        nc.gpsimd.tensor_scalar(x0_bf[:], x_raw[0][:].rearrange("p t c -> p c t"), 1.0, 0.0, MULT, ADD)
        quantize(x_mx[0], slice(0, J), x0_bf)
        wx_raw.append(load_rows("wx11", wx[K_PASS:L, half(1)], "w0_bf16"))
        quantize(wx_mx[0], slice(0, N), interleave("wx0", wx_raw[0], on_vector))
        x1_bf = [interleave("x1%d" % h, x_raw[1][:, :, half(h)], (on_vector, on_scalar)[h]) for h in range(2)]
        quantize(x_mx[1], half(0), x1_bf[0])
        wx10_bf = interleave("wx10", wx_raw[1], on_vector)
        quantize(x_mx[1], half(1), x1_bf[1])
        quantize(wx_mx[1], half(0), wx10_bf)
        quantize(wx_mx[1], half(1), interleave("wx11", wx_raw[2], on_vector))

        interp = []
        for nb in range(BLOCKS):
            held = keep.tile([P, J], F32, name="interp%d" % nb)
            nc.scalar.copy(held[:], total[nb][:])
            interp.append(held)

        accs = [prods.tile([P, J], F32, name="prod") for nb in range(BLOCKS)]
        for a in range(2):
            for nb in range(BLOCKS):
                product(accs[nb][:], wx_mx[a], block(nb), x_mx[a], slice(0, J), a == 0, a == 1)
        for nb, js in ((0, slice(0, J)), (1, slice(0, J)), (2, slice(0, J)), (3, half(0)), (3, half(1))):
            both = ring.tile([P, js.stop - js.start], F32, name="both")
            nc.vector.tensor_tensor(both[:], accs[nb][:, js], interp[nb][:, js], ADD)
            result = ring.tile([P, js.stop - js.start], F32, name="result", bufs=6)
            nc.scalar.activation(result[:], both[:], ACT.Gelu_apprx_tanh, bias=weight(G, nb))
            nc.sync.dma_start(out=out[block(nb), js], in_=result[:])
